import numpy as np
import ml_dtypes


def mxq(x, axis, fmt="e4m3"):
    dtype, down = {"e4m3": (ml_dtypes.float8_e4m3fn, 7), "e5m2": (ml_dtypes.float8_e5m2, 14)}[fmt]
    v = np.moveaxis(np.asarray(x, np.float32).astype(ml_dtypes.bfloat16).astype(np.float64), axis, -1)
    blocks = v.reshape(v.shape[:-1] + (-1, 32))
    amax = np.abs(blocks).max(-1, keepdims=True)
    byte = np.maximum(np.where(amax > 0, np.frexp(amax)[1] - 1 + 127, 0) - down, 1)
    scale = np.exp2(byte - 127.0)
    codes = (blocks / scale).astype(np.float32).astype(dtype).astype(np.float64)
    return np.moveaxis((codes * scale).reshape(v.shape), -1, axis)


WIDE = False


def mx_kscale(k):
    if not WIDE:
        return np.ones(k)
    levels = np.array([10, -10, 5, -5, 0])
    if k % 512:
        return np.exp2(np.random.permutation(np.resize(levels, k // 32))).repeat(32)
    a = np.empty((k // 512, 16))
    for p in range(k // 512):
        a[p, :8] = np.random.permutation(np.resize(levels, 8))
        for g in range(8):
            far = levels[np.abs(levels - a[p, g]) >= 10]
            a[p, g + 8] = far[np.random.randint(len(far))]
    return np.exp2(a.ravel()).repeat(32)


def f64(x):
    return np.asarray(x).astype(np.float64)


def striped(idx):
    return np.tile(np.asarray(idx).reshape(-1, 16).T, (8, 1)).astype(np.uint16)


def unstriped(offs):
    return offs[:16].T.reshape(-1).astype(np.int64)


E2M1 = np.array([0.0, 0.5, 1.0, 1.5, 2.0, 3.0, 4.0, 6.0, -0.0, -0.5, -1.0, -1.5, -2.0, -3.0, -4.0, -6.0])


def pack_weight(w, fmt):
    k, n = w.shape
    w = f64(np.asarray(w, np.float32).astype(ml_dtypes.bfloat16)).reshape(k // 32, 32, n)
    amax = np.abs(w).max(1)
    if fmt == "e4m3":
        byte = np.frexp(amax)[1] - 1 + 127 - 7
    else:
        mant, ex = np.frexp(amax / 6.0)
        byte = np.where(mant > 0.5, ex, ex - 1) + 127
    byte = np.clip(np.where(amax > 0, byte, 1), 1, 254)
    scaled = (w * np.exp2(127.0 - byte)[:, None, :]).reshape(k, n).astype(np.float32)
    by_word = np.ascontiguousarray(scaled.reshape(k // 512, 128, 4, n).transpose(0, 1, 3, 2))
    if fmt == "e4m3":
        words = by_word.astype(ml_dtypes.float8_e4m3fn).view(np.uint8)
    else:
        c = by_word.astype(ml_dtypes.float4_e2m1fn).view(np.uint8) & 0xF
        words = (c[..., 0::2] | (c[..., 1::2] << 4)).reshape(k // 512, 128, 2 * n)
    return np.ascontiguousarray(words), np.ascontiguousarray(byte.astype(np.uint8).reshape(k // 512, 16, n))


def unpack_weight(words, scales, fmt):
    g, _, n = scales.shape
    words = np.ascontiguousarray(words).reshape(g, 128, n, -1)
    if fmt == "e4m3":
        vals = words.view(ml_dtypes.float8_e4m3fn).astype(np.float64)
    else:
        nib = np.empty((g, 128, n, 4), np.uint8)
        nib[..., 0::2] = words & 0xF
        nib[..., 1::2] = words >> 4
        vals = E2M1[nib]
    vals = vals * np.repeat(np.exp2(scales.astype(np.float64) - 127.0), 8, axis=1)[..., None]
    return vals.transpose(0, 1, 3, 2).reshape(g * 512, n)


def sigmoid(v):
    return 1.0 / (1.0 + np.exp(-v))


D, E, T, I, Q, G = 512, 512, 2048, 512, 128, 32


def setup_inputs():
    n = np.random.standard_normal
    idx = np.random.permutation(T)[:I]
    fd = mx_kscale(D)
    fi = mx_kscale(I)
    ti = np.ones(T)
    ti[idx] = fi
    keysp = pack_weight(n((D, T)) / fd[:, None], "e4m3")
    return {
        "query": (n((D, Q)) * 0.5 / np.sqrt(D) * fd[:, None]).astype(np.float32),
        "dquery": (n((D, Q)) * 0.6 / np.sqrt(D) * fd[:, None]).astype(np.float32),
        "keys_words": keysp[0],
        "keys_scales": keysp[1],
        "th": (np.random.uniform(-0.2, 0.2, (Q, 1))).astype(np.float32),
        "steep": (np.random.uniform(2.0, 8.0, (Q, 1))).astype(np.float32),
        "os": (np.random.uniform(4.0, 16.0, (1, I)) * fi).astype(np.float32),
        "vals": (n((E, T)) / ti).astype(np.float32),
        "offs": striped(idx),
    }


def reference(query, dquery, keys_words, keys_scales, th, steep, os, vals, offs):
    idx = unstriped(offs)
    keysu = unpack_weight(keys_words, keys_scales, "e4m3")
    queryq = mxq(f64(query), 0, "e4m3")
    keysidxg = keysu[:, idx]
    a = queryq.T @ keysidxg
    dqueryq = mxq(f64(dquery), 0, "e4m3")
    ta = dqueryq.T @ keysidxg
    s = a.reshape(Q, G, I // G).mean(axis=2)
    gt = sigmoid((s - f64(th)) * f64(steep))
    gr = np.repeat(gt, I // G, axis=1)
    r = np.exp(a - np.max(a, axis=1, keepdims=True))
    p = r * gr
    ts = ta.reshape(Q, G, I // G).mean(axis=2)
    tgt = ts * f64(steep) * gt * (1.0 - gt)
    tgr = np.repeat(tgt, I // G, axis=1)
    tr = ta * r
    tp = tr * gr + tgr * r
    tw = (tp - np.sum(tp, axis=1, keepdims=True) * p / np.sum(p, axis=1, keepdims=True)) / np.sum(p, axis=1, keepdims=True)
    wo1 = tw * f64(os)
    wt1 = wo1.T
    vt1 = f64(vals)[:, idx].T
    wt1q = mxq(wt1, 0, "e4m3")
    vt1q = mxq(vt1, 0, "e4m3")
    o = wt1q.T @ vt1q
    return o

@@ -1,0 +1,190 @@
+from contextlib import ExitStack
+
+import concourse.mybir as mybir
+from concourse.masks import make_identity
+
+F32 = mybir.dt.float32
+BF16 = mybir.dt.bfloat16
+I32 = mybir.dt.int32
+U32 = mybir.dt.uint32
+U16 = mybir.dt.uint16
+U8 = mybir.dt.uint8
+FP8X4 = mybir.dt.float8_e4m3fn_x4
+ALU = mybir.AluOpType
+ACT = mybir.ActivationFunctionType
+AX = mybir.AxisListType
+
+P = 128
+PACK = 4
+D, E, T, I, Q, G = 512, 512, 2048, 512, 128, 32
+PAGE = I // G
+PLANES = E // P
+
+FLOPS = 2 * (2 * D * Q * I + I * Q * E)
+
+
+def tile_attend_ttpagegate_kernel(tc, query, dquery, keys_words, keys_scales, th, steep, slot_factor, vals, offs, out):
+    nc = tc.nc
+    with ExitStack() as ctx:
+        keep = ctx.enter_context(tc.tile_pool(name="keep", bufs=1))
+        psum = ctx.enter_context(tc.psum_pool(name="psum", bufs=1))
+
+        offsets = keep.tile([P, I // 16], U16, name="offsets")
+        nc.sync.dma_start(offsets[:], offs)
+
+        key_scales = keep.tile([P, T], U8, name="key_scales", align_bytes=64)
+        nc.vector.memset(key_scales[:].bitcast(I32), 0)
+        for quad in range(4):
+            nc.scalar.dma_start(
+                key_scales[32 * quad : 32 * quad + 4, :].bitcast(I32),
+                keys_scales[0, 4 * quad : 4 * quad + 4, :].bitcast(I32),
+            )
+        key_words = keep.tile([P, T], I32, name="key_words", align_bytes=64)
+        nc.sync.dma_start(key_words[:], keys_words[0].rearrange("p n t -> p (n t)").bitcast(I32))
+
+        raw_q = []
+        for name, src in (("query", query), ("dquery", dquery)):
+            raw = keep.tile([P, PACK, Q], F32, name="raw_" + name, align_bytes=64)
+            nc.sync.dma_start(raw[:], src.rearrange("(p t) q -> p t q", t=PACK))
+            raw_q.append(raw)
+
+        pools = []
+        for j in range(PLANES):
+            pool_j = keep.tile([P, T], F32, name="vals%d" % j, align_bytes=64)
+            nc.sync.dma_start(pool_j[:], vals[j * P : (j + 1) * P, :])
+            pools.append(pool_j)
+
+        th_col = keep.tile([P, 1], F32, name="th_col")
+        steep_col = keep.tile([P, 1], F32, name="steep_col")
+        os_cols = keep.tile([P, PACK], F32, name="os_cols")
+        nc.gpsimd.dma_start(steep_col[:], steep)
+        nc.gpsimd.dma_start(th_col[:], th)
+        nc.gpsimd.dma_start(os_cols[:], slot_factor.rearrange("o (p t) -> p (o t)", t=PACK))
+
+        one = keep.tile([P, 1], F32, name="one")
+        nc.vector.memset(one[:], 1.0)
+        warm = keep.tile([P, 1], F32, name="warm")
+        nc.scalar.activation(warm[:], one[:], ACT.Exp)
+
+        ident = keep.tile([P, P], F32, name="ident")
+        make_identity(nc, ident[:])
+
+        k_scales = keep.tile([P, I], U8, name="k_scales", align_bytes=64)
+        nc.vector.tensor_copy(k_scales[:], key_scales[:].indirect(offsets[:]))
+        k_codes = keep.tile([P, I], U32, name="k_codes", align_bytes=64)
+        nc.vector.tensor_copy(k_codes[:], key_words[:].bitcast(U32).indirect(offsets[:]))
+
+        slope = keep.tile([P, 1], F32, name="slope")
+        nc.vector.tensor_scalar(slope[:], steep_col[:], -1.0 / PAGE, None, ALU.mult)
+        shift = keep.tile([P, 1], F32, name="shift")
+        nc.vector.tensor_tensor(shift[:], steep_col[:], th_col[:], ALU.mult)
+
+        os_rows = psum.tile([P, PACK, P], F32, name="os_rows")
+        for t in range(PACK):
+            nc.tensor.transpose(os_rows[:, t, :], os_cols[:, t : t + 1].to_broadcast([P, P]), ident[:])
+
+        scores = []
+        for n, raw in enumerate(raw_q):
+            grouped = keep.tile([P, Q, PACK], BF16, name="q_grouped%d" % n, align_bytes=64)
+            nc.scalar.copy(
+                grouped[:].rearrange("p (c i) t -> p c t i", i=4),
+                raw[:].rearrange("p t (c i) -> p c t i", i=4),
+            )
+            codes = keep.tile([P, Q], U32, name="q_codes%d" % n, align_bytes=64)
+            scales = keep.tile([P, Q], U8, name="q_scales%d" % n, align_bytes=64)
+            nc.vector.quantize_mx(codes[:].bitcast(FP8X4), scales[:], grouped[:].rearrange("p q t -> p (q t)"))
+            acc = psum.tile([P, I], F32, name="score%d" % n)
+            nc.tensor.matmul_mx(
+                acc[:], lhsT=codes[:].bitcast(FP8X4), lhsT_scale=scales[:],
+                rhs=k_codes[:].bitcast(FP8X4), rhs_scale=k_scales[:], start=True, stop=True,
+            )
+            scores.append(acc)
+        a, ta = scores
+
+        v_codes = keep.tile([P, E], U32, name="v_codes", align_bytes=64)
+        v_scales = keep.tile([P, E], U8, name="v_scales", align_bytes=64)
+
+        def turn(rows, name, tag):
+            words = rows[:].bitcast(F32)
+            turned = psum.tile([P, 2, P], F32, name="turned_" + name, tag=tag)
+            for u in range(2):
+                nc.tensor.transpose(turned[:, u, :], words[:, u : I // 2 : 2], ident[:])
+            grouped = keep.tile([P, P * PACK], BF16, name="grouped_" + name, align_bytes=64)
+            nc.scalar.copy(
+                grouped[:].bitcast(F32).rearrange("p (c u) -> p c u", u=2),
+                turned[:].rearrange("p u c -> p c u"),
+            )
+            return grouped
+
+        def gather_vals(j):
+            picked = keep.tile([P, I], BF16, name="picked%d" % j, align_bytes=64)
+            nc.vector.tensor_copy(picked[:], pools[j][:].indirect(offsets[:]))
+            return turn(picked, "v%d" % j, "turned_v%d" % (j % 2))
+
+        def quantize_vals(j, grouped):
+            cols = slice(j * P, (j + 1) * P)
+            nc.vector.quantize_mx(v_codes[:, cols].bitcast(FP8X4), v_scales[:, cols], grouped[:])
+
+        def paged(ap):
+            return ap.rearrange("p (g j) -> p g j", j=PAGE)
+
+        def spread(ap):
+            return ap.unsqueeze(2).to_broadcast([P, G, PAGE])
+
+        neg_max = keep.tile([P, 1], F32, name="neg_max")
+        nc.vector.tensor_reduce(neg_max[:], a[:], AX.X, ALU.max, negate=True)
+        page_sum = keep.tile([P, G], F32, name="page_sum")
+        nc.vector.tensor_reduce(page_sum[:], paged(a[:]), AX.X, ALU.add)
+        dpage_sum = keep.tile([P, G], F32, name="dpage_sum")
+        nc.vector.tensor_reduce(dpage_sum[:], paged(ta[:]), AX.X, ALU.add)
+
+        r = keep.tile([P, I], F32, name="r")
+        nc.scalar.activation(r[:], a[:], ACT.Exp, bias=neg_max[:], scale=1.0)
+        odds = keep.tile([P, G], F32, name="odds")
+        nc.scalar.activation(odds[:], page_sum[:], ACT.Exp, bias=shift[:], scale=slope[:])
+        denom = keep.tile([P, G], F32, name="denom")
+        nc.scalar.activation(denom[:], odds[:], ACT.Identity, bias=one[:], scale=1.0)
+
+        g0 = gather_vals(0)
+        gate = keep.tile([P, G], F32, name="gate")
+        nc.vector.reciprocal(gate[:], denom[:])
+        quantize_vals(0, g0)
+        p = keep.tile([P, I], F32, name="p")
+        p_sum = keep.tile([P, 1], F32, name="p_sum")
+        nc.vector.scalar_tensor_tensor(paged(p[:]), paged(r[:]), 1.0, spread(gate[:]), ALU.mult, ALU.mult, accum_out=p_sum[:])
+        dgate = keep.tile([P, G], F32, name="dgate")
+        nc.vector.scalar_tensor_tensor(dgate[:], gate[:], 1.0, dpage_sum[:], ALU.subtract, ALU.mult)
+        inv_sum = keep.tile([P, 1], F32, name="inv_sum")
+        nc.vector.reciprocal(inv_sum[:], p_sum[:])
+        z = keep.tile([P, I], F32, name="z")
+        nc.vector.scalar_tensor_tensor(paged(z[:]), spread(dgate[:]), slope[:], paged(ta[:]), ALU.mult, ALU.add)
+        g1 = gather_vals(1)
+        tp = keep.tile([P, I], F32, name="tp")
+        mean_z = keep.tile([P, 1], F32, name="mean_z")
+        nc.vector.scalar_tensor_tensor(tp[:], z[:], inv_sum[:], p[:], ALU.mult, ALU.mult, accum_out=mean_z[:])
+        p_os = keep.tile([P, I], F32, name="p_os")
+        nc.vector.scalar_tensor_tensor(
+            p_os[:].rearrange("q (p t) -> q p t", t=PACK), p[:].rearrange("q (p t) -> q p t", t=PACK), inv_sum[:],
+            os_rows[:].rearrange("q t p -> q p t"), ALU.mult, ALU.mult,
+        )
+        quantize_vals(1, g1)
+        w = keep.tile([P, I], BF16, name="w", align_bytes=64)
+        nc.vector.scalar_tensor_tensor(w[:], z[:], mean_z[:], p_os[:], ALU.subtract, ALU.mult)
+        gw = turn(w, "w", "turned_w")
+        g2 = gather_vals(2)
+        w_codes = keep.tile([P, Q], U32, name="w_codes", align_bytes=64)
+        w_scales = keep.tile([P, Q], U8, name="w_scales", align_bytes=64)
+        nc.vector.quantize_mx(w_codes[:].bitcast(FP8X4), w_scales[:], gw[:])
+        g3 = gather_vals(3)
+        quantize_vals(2, g2)
+        quantize_vals(3, g3)
+
+        for n, (lo, hi, tag) in enumerate(((0, 256, "score0"), (256, 384, "score1"), (384, 512, "out_last"))):
+            acc = psum.tile([P, hi - lo], F32, name="out%d" % n, tag=tag)
+            nc.tensor.matmul_mx(
+                acc[:], lhsT=w_codes[:].bitcast(FP8X4), lhsT_scale=w_scales[:],
+                rhs=v_codes[:, lo:hi].bitcast(FP8X4), rhs_scale=v_scales[:, lo:hi], start=True, stop=True,
+            )
+            res = keep.tile([P, hi - lo], F32, name="res%d" % n)
+            nc.scalar.copy(res[:], acc[:])
+            nc.sync.dma_start(out[:, lo:hi], res[:])

@@ -1,7 +1,6 @@
 from contextlib import ExitStack
 
 import concourse.mybir as mybir
-from concourse.masks import make_identity
 
 F32 = mybir.dt.float32
 BF16 = mybir.dt.bfloat16
@@ -27,103 +26,115 @@ def tile_attend_ttpagegate_kernel(tc, query, dquery, keys_words, keys_scales, th
     nc = tc.nc
     with ExitStack() as ctx:
         keep = ctx.enter_context(tc.tile_pool(name="keep", bufs=1))
+        late = ctx.enter_context(tc.tile_pool(name="late", bufs=1))
         psum = ctx.enter_context(tc.psum_pool(name="psum", bufs=1))
 
         offsets = keep.tile([P, I // 16], U16, name="offsets")
         nc.sync.dma_start(offsets[:], offs)
 
         key_scales = keep.tile([P, T], U8, name="key_scales", align_bytes=64)
-        nc.vector.memset(key_scales[:].bitcast(I32), 0)
+        nc.gpsimd.memset(key_scales[:].bitcast(I32), 0)
         for quad in range(4):
-            nc.scalar.dma_start(
+            nc.sync.dma_start(
                 key_scales[32 * quad : 32 * quad + 4, :].bitcast(I32),
                 keys_scales[0, 4 * quad : 4 * quad + 4, :].bitcast(I32),
             )
-        key_words = keep.tile([P, T], I32, name="key_words", align_bytes=64)
-        nc.sync.dma_start(key_words[:], keys_words[0].rearrange("p n t -> p (n t)").bitcast(I32))
 
-        raw_q = []
-        for name, src in (("query", query), ("dquery", dquery)):
-            raw = keep.tile([P, PACK, Q], F32, name="raw_" + name, align_bytes=64)
-            nc.sync.dma_start(raw[:], src.rearrange("(p t) q -> p t q", t=PACK))
-            raw_q.append(raw)
+        row_bytes = 4 * T
+        ones = late.tile([P, (PLANES + 2) * T], F32, name="ones", offset=0)
+        nc.gpsimd.memset(ones[:, 0:P], 1.0)
+        ident = keep.tile([P, P], F32, name="ident")
+        nc.gpsimd.affine_select(
+            out=ident[:], in_=ones[:, 0:P], compare_op=ALU.is_equal, fill=0.0, base=0,
+            pattern=[[-1, P]], channel_multiplier=1,
+        )
+
+        key_words = late.tile([P, T], I32, name="key_words", offset=PLANES * row_bytes)
+        nc.sync.dma_start(key_words[:], keys_words[0].rearrange("p n t -> p (n t)").bitcast(I32))
+        raw_q = late.tile([P, PACK, Q], F32, name="raw_q", offset=(PLANES + 1) * row_bytes)
+        nc.sync.dma_start(raw_q[:], query.rearrange("(p t) q -> p t q", t=PACK))
+        raw_dq = late.tile([P, PACK, Q], F32, name="raw_dq", offset=(PLANES + 1) * row_bytes + 4 * PACK * Q)
+        nc.sync.dma_start(raw_dq[:], dquery.rearrange("(p t) q -> p t q", t=PACK))
+
+        small = (PLANES + 1) * row_bytes + 8 * PACK * Q
+        steep_col = late.tile([P, 1], F32, name="steep_col", offset=small)
+        nc.sync.dma_start(steep_col[:], steep)
+        th_col = late.tile([P, 1], F32, name="th_col", offset=small + 32)
+        nc.sync.dma_start(th_col[:], th)
 
         pools = []
+        os_cols = late.tile([P, PACK], F32, name="os_cols", offset=small + 64)
         for j in range(PLANES):
-            pool_j = keep.tile([P, T], F32, name="vals%d" % j, align_bytes=64)
+            pool_j = late.tile([P, T], F32, name="vals%d" % j, offset=j * row_bytes)
             nc.sync.dma_start(pool_j[:], vals[j * P : (j + 1) * P, :])
             pools.append(pool_j)
-
-        th_col = keep.tile([P, 1], F32, name="th_col")
-        steep_col = keep.tile([P, 1], F32, name="steep_col")
-        os_cols = keep.tile([P, PACK], F32, name="os_cols")
-        nc.gpsimd.dma_start(steep_col[:], steep)
-        nc.gpsimd.dma_start(th_col[:], th)
-        nc.gpsimd.dma_start(os_cols[:], slot_factor.rearrange("o (p t) -> p (o t)", t=PACK))
+            if j == 0:
+                nc.sync.dma_start(os_cols[:], slot_factor.rearrange("o (p t) -> p (o t)", t=PACK))
 
         one = keep.tile([P, 1], F32, name="one")
         nc.vector.memset(one[:], 1.0)
         warm = keep.tile([P, 1], F32, name="warm")
         nc.scalar.activation(warm[:], one[:], ACT.Exp)
 
-        ident = keep.tile([P, P], F32, name="ident")
-        make_identity(nc, ident[:])
+        def interleave(copy, raw, name):
+            grouped = keep.tile([P, Q, PACK], BF16, name=name, align_bytes=64)
+            copy(
+                grouped[:].rearrange("p (c i) t -> p c t i", i=4),
+                raw[:].rearrange("p t (c i) -> p c t i", i=4),
+            )
+            return grouped[:].rearrange("p q t -> p (q t)")
 
+        def quantize(grouped, width, name, offset=None):
+            if offset is None:
+                codes = keep.tile([P, width], U32, name=name + "_codes", align_bytes=64)
+            else:
+                codes = late.tile([P, width], U32, name=name + "_codes", align_bytes=64, offset=offset)
+            scales = keep.tile([P, width], U8, name=name + "_scales", align_bytes=64)
+            nc.vector.quantize_mx(codes[:].bitcast(FP8X4), scales[:], grouped)
+            return codes, scales
+
+        def product(acc, stationary, moving):
+            nc.tensor.matmul_mx(
+                acc, lhsT=stationary[0][:].bitcast(FP8X4), lhsT_scale=stationary[1][:],
+                rhs=moving[0][:].bitcast(FP8X4), rhs_scale=moving[1][:], start=True, stop=True,
+            )
+
+        q_grouped = interleave(nc.scalar.copy, raw_q, "q_grouped")
+        dq_grouped = interleave(nc.scalar.copy, raw_dq, "dq_grouped")
         k_scales = keep.tile([P, I], U8, name="k_scales", align_bytes=64)
         nc.vector.tensor_copy(k_scales[:], key_scales[:].indirect(offsets[:]))
         k_codes = keep.tile([P, I], U32, name="k_codes", align_bytes=64)
         nc.vector.tensor_copy(k_codes[:], key_words[:].bitcast(U32).indirect(offsets[:]))
-
+        q_mx = quantize(q_grouped, Q, "q", PLANES * row_bytes)
+        dq_mx = quantize(dq_grouped, Q, "dq", PLANES * row_bytes + 4 * Q)
         slope = keep.tile([P, 1], F32, name="slope")
-        nc.vector.tensor_scalar(slope[:], steep_col[:], -1.0 / PAGE, None, ALU.mult)
+        nc.scalar.activation(slope[:], steep_col[:], ACT.Copy, scale=-1.0 / PAGE)
         shift = keep.tile([P, 1], F32, name="shift")
-        nc.vector.tensor_tensor(shift[:], steep_col[:], th_col[:], ALU.mult)
+        nc.scalar.activation(shift[:], th_col[:], ACT.Copy, scale=steep_col[:])
+
+        a = psum.tile([P, I], F32, name="a")
+        product(a[:], q_mx, (k_codes, k_scales))
+        ta = psum.tile([P, I], F32, name="ta")
+        product(ta[:], dq_mx, (k_codes, k_scales))
 
         os_rows = psum.tile([P, PACK, P], F32, name="os_rows")
         for t in range(PACK):
             nc.tensor.transpose(os_rows[:, t, :], os_cols[:, t : t + 1].to_broadcast([P, P]), ident[:])
 
-        scores = []
-        for n, raw in enumerate(raw_q):
-            grouped = keep.tile([P, Q, PACK], BF16, name="q_grouped%d" % n, align_bytes=64)
-            nc.scalar.copy(
-                grouped[:].rearrange("p (c i) t -> p c t i", i=4),
-                raw[:].rearrange("p t (c i) -> p c t i", i=4),
-            )
-            codes = keep.tile([P, Q], U32, name="q_codes%d" % n, align_bytes=64)
-            scales = keep.tile([P, Q], U8, name="q_scales%d" % n, align_bytes=64)
-            nc.vector.quantize_mx(codes[:].bitcast(FP8X4), scales[:], grouped[:].rearrange("p q t -> p (q t)"))
-            acc = psum.tile([P, I], F32, name="score%d" % n)
-            nc.tensor.matmul_mx(
-                acc[:], lhsT=codes[:].bitcast(FP8X4), lhsT_scale=scales[:],
-                rhs=k_codes[:].bitcast(FP8X4), rhs_scale=k_scales[:], start=True, stop=True,
-            )
-            scores.append(acc)
-        a, ta = scores
-
-        v_codes = keep.tile([P, E], U32, name="v_codes", align_bytes=64)
-        v_scales = keep.tile([P, E], U8, name="v_scales", align_bytes=64)
-
-        def turn(rows, name, tag):
+        def turn(rows, grouped, name, tag, copy=nc.scalar.copy):
             words = rows[:].bitcast(F32)
             turned = psum.tile([P, 2, P], F32, name="turned_" + name, tag=tag)
             for u in range(2):
                 nc.tensor.transpose(turned[:, u, :], words[:, u : I // 2 : 2], ident[:])
-            grouped = keep.tile([P, P * PACK], BF16, name="grouped_" + name, align_bytes=64)
-            nc.scalar.copy(
-                grouped[:].bitcast(F32).rearrange("p (c u) -> p c u", u=2),
+            copy(
+                grouped.bitcast(F32).rearrange("p (c u) -> p c u", u=2),
                 turned[:].rearrange("p u c -> p c u"),
             )
-            return grouped
 
-        def gather_vals(j):
-            picked = keep.tile([P, I], BF16, name="picked%d" % j, align_bytes=64)
+        def gather_vals(j, grouped, tag, copy=nc.scalar.copy):
+            picked = keep.tile([P, I], BF16, name="picked%d" % j, tag=tag, align_bytes=64)
             nc.vector.tensor_copy(picked[:], pools[j][:].indirect(offsets[:]))
-            return turn(picked, "v%d" % j, "turned_v%d" % (j % 2))
-
-        def quantize_vals(j, grouped):
-            cols = slice(j * P, (j + 1) * P)
-            nc.vector.quantize_mx(v_codes[:, cols].bitcast(FP8X4), v_scales[:, cols], grouped[:])
+            turn(picked, grouped, "v%d" % j, "turned_v%d" % j, copy)
 
         def paged(ap):
             return ap.rearrange("p (g j) -> p g j", j=PAGE)
@@ -131,60 +142,67 @@ def tile_attend_ttpagegate_kernel(tc, query, dquery, keys_words, keys_scales, th
         def spread(ap):
             return ap.unsqueeze(2).to_broadcast([P, G, PAGE])
 
-        neg_max = keep.tile([P, 1], F32, name="neg_max")
-        nc.vector.tensor_reduce(neg_max[:], a[:], AX.X, ALU.max, negate=True)
+        v01_grouped = keep.tile([P, 2 * I], BF16, name="v01_grouped", align_bytes=64)
+        v2_grouped = keep.tile([P, I], BF16, name="v2_grouped", align_bytes=64)
+        v3_grouped = keep.tile([P, I], BF16, name="v3_grouped", align_bytes=64)
+        w_grouped = keep.tile([P, I], BF16, name="w_grouped", align_bytes=64)
+
         page_sum = keep.tile([P, G], F32, name="page_sum")
         nc.vector.tensor_reduce(page_sum[:], paged(a[:]), AX.X, ALU.add)
-        dpage_sum = keep.tile([P, G], F32, name="dpage_sum")
-        nc.vector.tensor_reduce(dpage_sum[:], paged(ta[:]), AX.X, ALU.add)
+        neg_max = keep.tile([P, 1], F32, name="neg_max", tag="cast0", align_bytes=64)
+        nc.vector.tensor_reduce(neg_max[:], a[:], AX.X, ALU.max, negate=True)
 
-        r = keep.tile([P, I], F32, name="r")
-        nc.scalar.activation(r[:], a[:], ACT.Exp, bias=neg_max[:], scale=1.0)
         odds = keep.tile([P, G], F32, name="odds")
         nc.scalar.activation(odds[:], page_sum[:], ACT.Exp, bias=shift[:], scale=slope[:])
-        denom = keep.tile([P, G], F32, name="denom")
+        denom = keep.tile([P, G], F32, name="denom", tag="slot0", align_bytes=64)
         nc.scalar.activation(denom[:], odds[:], ACT.Identity, bias=one[:], scale=1.0)
+        r = keep.tile([P, I], F32, name="r")
+        nc.scalar.activation(r[:], a[:], ACT.Exp, bias=neg_max[:], scale=1.0)
 
-        g0 = gather_vals(0)
+        cast0 = keep.tile([P, T], BF16, name="cast0", tag="cast0", align_bytes=64)
+        for c in range(0, T, 512):
+            nc.scalar.activation(cast0[:, c : c + 512], pools[0][:, c : c + 512], ACT.Copy)
+        picked0 = keep.tile([P, I], BF16, name="picked0", align_bytes=64)
+        nc.scalar.activation(picked0[:], cast0[:].indirect(offsets[:]), ACT.Copy)
+
         gate = keep.tile([P, G], F32, name="gate")
         nc.vector.reciprocal(gate[:], denom[:])
-        quantize_vals(0, g0)
-        p = keep.tile([P, I], F32, name="p")
+        dpage_sum = keep.tile([P, G], F32, name="dpage_sum", tag="slot0", align_bytes=64)
+        nc.vector.tensor_reduce(dpage_sum[:], paged(ta[:]), AX.X, ALU.add)
+        p = keep.tile([P, I], F32, name="p", tag="slot1", align_bytes=64)
         p_sum = keep.tile([P, 1], F32, name="p_sum")
         nc.vector.scalar_tensor_tensor(paged(p[:]), paged(r[:]), 1.0, spread(gate[:]), ALU.mult, ALU.mult, accum_out=p_sum[:])
         dgate = keep.tile([P, G], F32, name="dgate")
         nc.vector.scalar_tensor_tensor(dgate[:], gate[:], 1.0, dpage_sum[:], ALU.subtract, ALU.mult)
         inv_sum = keep.tile([P, 1], F32, name="inv_sum")
         nc.vector.reciprocal(inv_sum[:], p_sum[:])
-        z = keep.tile([P, I], F32, name="z")
+        z = keep.tile([P, I], F32, name="z", tag="slot3", align_bytes=64)
         nc.vector.scalar_tensor_tensor(paged(z[:]), spread(dgate[:]), slope[:], paged(ta[:]), ALU.mult, ALU.add)
-        g1 = gather_vals(1)
-        tp = keep.tile([P, I], F32, name="tp")
-        mean_z = keep.tile([P, 1], F32, name="mean_z")
-        nc.vector.scalar_tensor_tensor(tp[:], z[:], inv_sum[:], p[:], ALU.mult, ALU.mult, accum_out=mean_z[:])
-        p_os = keep.tile([P, I], F32, name="p_os")
+        p_os = keep.tile([P, I], F32, name="p_os", tag="slot2", align_bytes=64)
         nc.vector.scalar_tensor_tensor(
             p_os[:].rearrange("q (p t) -> q p t", t=PACK), p[:].rearrange("q (p t) -> q p t", t=PACK), inv_sum[:],
             os_rows[:].rearrange("q t p -> q p t"), ALU.mult, ALU.mult,
         )
-        quantize_vals(1, g1)
+        tp = keep.tile([P, I], F32, name="tp")
+        mean_z = keep.tile([P, 1], F32, name="mean_z")
+        nc.vector.scalar_tensor_tensor(tp[:], z[:], inv_sum[:], p[:], ALU.mult, ALU.mult, accum_out=mean_z[:])
+        gather_vals(1, v01_grouped[:, I : 2 * I], "slot1")
+        turn(picked0, v01_grouped[:, 0:I], "v0", "turned_v1")
         w = keep.tile([P, I], BF16, name="w", align_bytes=64)
         nc.vector.scalar_tensor_tensor(w[:], z[:], mean_z[:], p_os[:], ALU.subtract, ALU.mult)
-        gw = turn(w, "w", "turned_w")
-        g2 = gather_vals(2)
-        w_codes = keep.tile([P, Q], U32, name="w_codes", align_bytes=64)
-        w_scales = keep.tile([P, Q], U8, name="w_scales", align_bytes=64)
-        nc.vector.quantize_mx(w_codes[:].bitcast(FP8X4), w_scales[:], gw[:])
-        g3 = gather_vals(3)
-        quantize_vals(2, g2)
-        quantize_vals(3, g3)
+        turn(w, w_grouped[:], "w", "turned_w")
+        gather_vals(2, v2_grouped[:], "slot2")
+        picked3 = keep.tile([P, I], BF16, name="picked3", tag="slot3", align_bytes=64)
+        nc.vector.tensor_copy(picked3[:], pools[3][:].indirect(offsets[:]))
+        w_mx = quantize(w_grouped[:], Q, "w", 3 * row_bytes)
+        v01_mx = quantize(v01_grouped[:], 2 * P, "v01", 3 * row_bytes + 1024)
+        v2_mx = quantize(v2_grouped[:], P, "v2", 3 * row_bytes + 2048)
+        turn(picked3, v3_grouped[:], "v3", "turned_v3", nc.vector.tensor_copy)
+        v3_mx = quantize(v3_grouped[:], P, "v3")
 
-        for n, (lo, hi, tag) in enumerate(((0, 256, "score0"), (256, 384, "score1"), (384, 512, "out_last"))):
-            acc = psum.tile([P, hi - lo], F32, name="out%d" % n, tag=tag)
-            nc.tensor.matmul_mx(
-                acc[:], lhsT=w_codes[:].bitcast(FP8X4), lhsT_scale=w_scales[:],
-                rhs=v_codes[:, lo:hi].bitcast(FP8X4), rhs_scale=v_scales[:, lo:hi], start=True, stop=True,
-            )
-            res = keep.tile([P, hi - lo], F32, name="res%d" % n)
+        for v_mx, lo, hi, tag in ((v01_mx, 0, 256, "a"), (v2_mx, 256, 384, "ta"), (v3_mx, 384, 512, "out_last")):
+            acc = psum.tile([P, hi - lo], F32, name="out%d" % lo, tag=tag)
+            product(acc[:], w_mx, v_mx)
+            res = keep.tile([P, hi - lo], F32, name="res%d" % lo)
             nc.scalar.copy(res[:], acc[:])
             nc.sync.dma_start(out[:, lo:hi], res[:])

@@ -31,6 +31,8 @@ def tile_attend_ttpagegate_kernel(tc, query, dquery, keys_words, keys_scales, th
 
         offsets = keep.tile([P, I // 16], U16, name="offsets")
         nc.sync.dma_start(offsets[:], offs)
+        raw_q = keep.tile([P, PACK, Q], F32, name="raw_q", align_bytes=64)
+        nc.sync.dma_start(raw_q[:], query.rearrange("(p t) q -> p t q", t=PACK))
 
         key_scales = keep.tile([P, T], U8, name="key_scales", align_bytes=64)
         nc.gpsimd.memset(key_scales[:].bitcast(I32), 0)
@@ -42,7 +44,7 @@ def tile_attend_ttpagegate_kernel(tc, query, dquery, keys_words, keys_scales, th
 
         row_bytes = 4 * T
         ones = late.tile([P, (PLANES + 2) * T], F32, name="ones", offset=0)
-        nc.gpsimd.memset(ones[:, 0:P], 1.0)
+        nc.vector.memset(ones[:, 0:P], 1.0)
         ident = keep.tile([P, P], F32, name="ident")
         nc.gpsimd.affine_select(
             out=ident[:], in_=ones[:, 0:P], compare_op=ALU.is_equal, fill=0.0, base=0,
@@ -51,8 +53,6 @@ def tile_attend_ttpagegate_kernel(tc, query, dquery, keys_words, keys_scales, th
 
         key_words = late.tile([P, T], I32, name="key_words", offset=PLANES * row_bytes)
         nc.sync.dma_start(key_words[:], keys_words[0].rearrange("p n t -> p (n t)").bitcast(I32))
-        raw_q = late.tile([P, PACK, Q], F32, name="raw_q", offset=(PLANES + 1) * row_bytes)
-        nc.sync.dma_start(raw_q[:], query.rearrange("(p t) q -> p t q", t=PACK))
         raw_dq = late.tile([P, PACK, Q], F32, name="raw_dq", offset=(PLANES + 1) * row_bytes + 4 * PACK * Q)
         nc.sync.dma_start(raw_dq[:], dquery.rearrange("(p t) q -> p t q", t=PACK))
 
@@ -93,27 +93,30 @@ def tile_attend_ttpagegate_kernel(tc, query, dquery, keys_words, keys_scales, th
             nc.vector.quantize_mx(codes[:].bitcast(FP8X4), scales[:], grouped)
             return codes, scales
 
-        def product(acc, stationary, moving):
+        def product(acc, stationary, moving, cols=slice(None)):
             nc.tensor.matmul_mx(
                 acc, lhsT=stationary[0][:].bitcast(FP8X4), lhsT_scale=stationary[1][:],
-                rhs=moving[0][:].bitcast(FP8X4), rhs_scale=moving[1][:], start=True, stop=True,
+                rhs=moving[0][:, cols].bitcast(FP8X4), rhs_scale=moving[1][:, cols], start=True, stop=True,
             )
 
         q_grouped = interleave(nc.scalar.copy, raw_q, "q_grouped")
         dq_grouped = interleave(nc.scalar.copy, raw_dq, "dq_grouped")
         k_scales = keep.tile([P, I], U8, name="k_scales", align_bytes=64)
         nc.vector.tensor_copy(k_scales[:], key_scales[:].indirect(offsets[:]))
+        q_mx = quantize(q_grouped, Q, "q")
         k_codes = keep.tile([P, I], U32, name="k_codes", align_bytes=64)
-        nc.vector.tensor_copy(k_codes[:], key_words[:].bitcast(U32).indirect(offsets[:]))
-        q_mx = quantize(q_grouped, Q, "q", PLANES * row_bytes)
+        halves = [slice(h * I // 2, (h + 1) * I // 2) for h in range(2)]
+        for h, cols in enumerate(halves):
+            nc.vector.tensor_copy(k_codes[:, cols], key_words[:].bitcast(U32).indirect(offsets[:, 16 * h : 16 * (h + 1)]))
         dq_mx = quantize(dq_grouped, Q, "dq", PLANES * row_bytes + 4 * Q)
         slope = keep.tile([P, 1], F32, name="slope")
         nc.scalar.activation(slope[:], steep_col[:], ACT.Copy, scale=-1.0 / PAGE)
         shift = keep.tile([P, 1], F32, name="shift")
         nc.scalar.activation(shift[:], th_col[:], ACT.Copy, scale=steep_col[:])
 
-        a = psum.tile([P, I], F32, name="a")
-        product(a[:], q_mx, (k_codes, k_scales))
+        a = [psum.tile([P, I // 2], F32, name="a%d" % h) for h in range(2)]
+        for h, cols in enumerate(halves):
+            product(a[h][:], q_mx, (k_codes, k_scales), cols)
         ta = psum.tile([P, I], F32, name="ta")
         product(ta[:], dq_mx, (k_codes, k_scales))
 
@@ -148,16 +151,23 @@ def tile_attend_ttpagegate_kernel(tc, query, dquery, keys_words, keys_scales, th
         w_grouped = keep.tile([P, I], BF16, name="w_grouped", align_bytes=64)
 
         page_sum = keep.tile([P, G], F32, name="page_sum")
-        nc.vector.tensor_reduce(page_sum[:], paged(a[:]), AX.X, ALU.add)
+        neg_max_first = keep.tile([P, 1], F32, name="neg_max_first")
         neg_max = keep.tile([P, 1], F32, name="neg_max", tag="cast0", align_bytes=64)
-        nc.vector.tensor_reduce(neg_max[:], a[:], AX.X, ALU.max, negate=True)
+        neg_a = keep.tile([P, I // 2], F32, name="neg_a")
+        nc.vector.tensor_reduce(page_sum[:, 0 : G // 2], paged(a[0][:]), AX.X, ALU.add)
+        nc.vector.tensor_reduce(neg_max_first[:], a[0][:], AX.X, ALU.max, negate=True)
+        nc.vector.tensor_reduce(page_sum[:, G // 2 : G], paged(a[1][:]), AX.X, ALU.add)
+        nc.vector.tensor_scalar(neg_a[:], a[1][:], -1.0, neg_max_first[:], ALU.mult, ALU.min, accum_out=neg_max[:])
+        dpage_sum = keep.tile([P, G], F32, name="dpage_sum")
+        nc.vector.tensor_reduce(dpage_sum[:], paged(ta[:]), AX.X, ALU.add)
 
         odds = keep.tile([P, G], F32, name="odds")
         nc.scalar.activation(odds[:], page_sum[:], ACT.Exp, bias=shift[:], scale=slope[:])
-        denom = keep.tile([P, G], F32, name="denom", tag="slot0", align_bytes=64)
+        denom = keep.tile([P, G], F32, name="denom")
         nc.scalar.activation(denom[:], odds[:], ACT.Identity, bias=one[:], scale=1.0)
-        r = keep.tile([P, I], F32, name="r")
-        nc.scalar.activation(r[:], a[:], ACT.Exp, bias=neg_max[:], scale=1.0)
+        r = keep.tile([P, I], F32, name="r", tag="slot0", align_bytes=64)
+        for h, cols in enumerate(halves):
+            nc.scalar.activation(r[:, cols], a[h][:], ACT.Exp, bias=neg_max[:], scale=1.0)
 
         cast0 = keep.tile([P, T], BF16, name="cast0", tag="cast0", align_bytes=64)
         for c in range(0, T, 512):
@@ -167,23 +177,21 @@ def tile_attend_ttpagegate_kernel(tc, query, dquery, keys_words, keys_scales, th
 
         gate = keep.tile([P, G], F32, name="gate")
         nc.vector.reciprocal(gate[:], denom[:])
-        dpage_sum = keep.tile([P, G], F32, name="dpage_sum", tag="slot0", align_bytes=64)
-        nc.vector.tensor_reduce(dpage_sum[:], paged(ta[:]), AX.X, ALU.add)
-        p = keep.tile([P, I], F32, name="p", tag="slot1", align_bytes=64)
+        p = keep.tile([P, I], F32, name="p", tag="slot2", align_bytes=64)
         p_sum = keep.tile([P, 1], F32, name="p_sum")
         nc.vector.scalar_tensor_tensor(paged(p[:]), paged(r[:]), 1.0, spread(gate[:]), ALU.mult, ALU.mult, accum_out=p_sum[:])
-        dgate = keep.tile([P, G], F32, name="dgate")
+        dgate = keep.tile([P, G], F32, name="dgate", tag="slot0", align_bytes=64)
         nc.vector.scalar_tensor_tensor(dgate[:], gate[:], 1.0, dpage_sum[:], ALU.subtract, ALU.mult)
         inv_sum = keep.tile([P, 1], F32, name="inv_sum")
         nc.vector.reciprocal(inv_sum[:], p_sum[:])
-        z = keep.tile([P, I], F32, name="z", tag="slot3", align_bytes=64)
+        z = keep.tile([P, I], F32, name="z")
         nc.vector.scalar_tensor_tensor(paged(z[:]), spread(dgate[:]), slope[:], paged(ta[:]), ALU.mult, ALU.add)
-        p_os = keep.tile([P, I], F32, name="p_os", tag="slot2", align_bytes=64)
+        p_os = keep.tile([P, I], F32, name="p_os")
         nc.vector.scalar_tensor_tensor(
             p_os[:].rearrange("q (p t) -> q p t", t=PACK), p[:].rearrange("q (p t) -> q p t", t=PACK), inv_sum[:],
             os_rows[:].rearrange("q t p -> q p t"), ALU.mult, ALU.mult,
         )
-        tp = keep.tile([P, I], F32, name="tp")
+        tp = keep.tile([P, I], F32, name="tp", tag="slot3", align_bytes=64)
         mean_z = keep.tile([P, 1], F32, name="mean_z")
         nc.vector.scalar_tensor_tensor(tp[:], z[:], inv_sum[:], p[:], ALU.mult, ALU.mult, accum_out=mean_z[:])
         gather_vals(1, v01_grouped[:, I : 2 * I], "slot1")
@@ -200,7 +208,7 @@ def tile_attend_ttpagegate_kernel(tc, query, dquery, keys_words, keys_scales, th
         turn(picked3, v3_grouped[:], "v3", "turned_v3", nc.vector.tensor_copy)
         v3_mx = quantize(v3_grouped[:], P, "v3")
 
-        for v_mx, lo, hi, tag in ((v01_mx, 0, 256, "a"), (v2_mx, 256, 384, "ta"), (v3_mx, 384, 512, "out_last")):
+        for v_mx, lo, hi, tag in ((v01_mx, 0, 256, "a0"), (v2_mx, 256, 384, "ta"), (v3_mx, 384, 512, "a1")):
             acc = psum.tile([P, hi - lo], F32, name="out%d" % lo, tag=tag)
             product(acc[:], w_mx, v_mx)
             res = keep.tile([P, hi - lo], F32, name="res%d" % lo)

from contextlib import ExitStack

import concourse.mybir as mybir

F32 = mybir.dt.float32
BF16 = mybir.dt.bfloat16
I32 = mybir.dt.int32
U32 = mybir.dt.uint32
U16 = mybir.dt.uint16
U8 = mybir.dt.uint8
FP8X4 = mybir.dt.float8_e4m3fn_x4
ALU = mybir.AluOpType
ACT = mybir.ActivationFunctionType
AX = mybir.AxisListType

P = 128
PACK = 4
D, E, T, I, Q, G = 512, 512, 2048, 512, 128, 32
PAGE = I // G
PLANES = E // P

FLOPS = 2 * (2 * D * Q * I + I * Q * E)


def tile_attend_ttpagegate_kernel(tc, query, dquery, keys_words, keys_scales, th, steep, slot_factor, vals, offs, out):
    nc = tc.nc
    with ExitStack() as ctx:
        keep = ctx.enter_context(tc.tile_pool(name="keep", bufs=1))
        late = ctx.enter_context(tc.tile_pool(name="late", bufs=1))
        psum = ctx.enter_context(tc.psum_pool(name="psum", bufs=1))

        offsets = keep.tile([P, I // 16], U16, name="offsets")
        nc.sync.dma_start(offsets[:], offs)
        raw_q = keep.tile([P, PACK, Q], F32, name="raw_q", align_bytes=64)
        nc.sync.dma_start(raw_q[:], query.rearrange("(p t) q -> p t q", t=PACK))

        key_scales = keep.tile([P, T], U8, name="key_scales", align_bytes=64)
        nc.gpsimd.memset(key_scales[:].bitcast(I32), 0)
        for quad in range(4):
            nc.sync.dma_start(
                key_scales[32 * quad : 32 * quad + 4, :].bitcast(I32),
                keys_scales[0, 4 * quad : 4 * quad + 4, :].bitcast(I32),
            )

        row_bytes = 4 * T
        ones = late.tile([P, (PLANES + 2) * T], F32, name="ones", offset=0)
        nc.vector.memset(ones[:, 0:P], 1.0)
        ident = keep.tile([P, P], F32, name="ident")
        nc.gpsimd.affine_select(
            out=ident[:], in_=ones[:, 0:P], compare_op=ALU.is_equal, fill=0.0, base=0,
            pattern=[[-1, P]], channel_multiplier=1,
        )

        key_words = late.tile([P, T], I32, name="key_words", offset=PLANES * row_bytes)
        nc.sync.dma_start(key_words[:], keys_words[0].rearrange("p n t -> p (n t)").bitcast(I32))
        raw_dq = late.tile([P, PACK, Q], F32, name="raw_dq", offset=(PLANES + 1) * row_bytes + 4 * PACK * Q)
        nc.sync.dma_start(raw_dq[:], dquery.rearrange("(p t) q -> p t q", t=PACK))

        small = (PLANES + 1) * row_bytes + 8 * PACK * Q
        steep_col = late.tile([P, 1], F32, name="steep_col", offset=small)
        nc.sync.dma_start(steep_col[:], steep)
        th_col = late.tile([P, 1], F32, name="th_col", offset=small + 32)
        nc.sync.dma_start(th_col[:], th)

        pools = []
        os_cols = late.tile([P, PACK], F32, name="os_cols", offset=small + 64)
        for j in range(PLANES):
            pool_j = late.tile([P, T], F32, name="vals%d" % j, offset=j * row_bytes)
            nc.sync.dma_start(pool_j[:], vals[j * P : (j + 1) * P, :])
            pools.append(pool_j)
            if j == 0:
                nc.sync.dma_start(os_cols[:], slot_factor.rearrange("o (p t) -> p (o t)", t=PACK))

        one = keep.tile([P, 1], F32, name="one")
        nc.vector.memset(one[:], 1.0)
        warm = keep.tile([P, 1], F32, name="warm")
        nc.scalar.activation(warm[:], one[:], ACT.Exp)

        def interleave(copy, raw, name):
            grouped = keep.tile([P, Q, PACK], BF16, name=name, align_bytes=64)
            copy(
                grouped[:].rearrange("p (c i) t -> p c t i", i=4),
                raw[:].rearrange("p t (c i) -> p c t i", i=4),
            )
            return grouped[:].rearrange("p q t -> p (q t)")

        def quantize(grouped, width, name, offset=None):
            if offset is None:
                codes = keep.tile([P, width], U32, name=name + "_codes", align_bytes=64)
            else:
                codes = late.tile([P, width], U32, name=name + "_codes", align_bytes=64, offset=offset)
            scales = keep.tile([P, width], U8, name=name + "_scales", align_bytes=64)
            nc.vector.quantize_mx(codes[:].bitcast(FP8X4), scales[:], grouped)
            return codes, scales

        def product(acc, stationary, moving, cols=slice(None)):
            nc.tensor.matmul_mx(
                acc, lhsT=stationary[0][:].bitcast(FP8X4), lhsT_scale=stationary[1][:],
                rhs=moving[0][:, cols].bitcast(FP8X4), rhs_scale=moving[1][:, cols], start=True, stop=True,
            )

        q_grouped = interleave(nc.scalar.copy, raw_q, "q_grouped")
        dq_grouped = interleave(nc.scalar.copy, raw_dq, "dq_grouped")
        k_scales = keep.tile([P, I], U8, name="k_scales", align_bytes=64)
        nc.vector.tensor_copy(k_scales[:], key_scales[:].indirect(offsets[:]))
        q_mx = quantize(q_grouped, Q, "q")
        k_codes = keep.tile([P, I], U32, name="k_codes", align_bytes=64)
        halves = [slice(h * I // 2, (h + 1) * I // 2) for h in range(2)]
        for h, cols in enumerate(halves):
            nc.vector.tensor_copy(k_codes[:, cols], key_words[:].bitcast(U32).indirect(offsets[:, 16 * h : 16 * (h + 1)]))
        dq_mx = quantize(dq_grouped, Q, "dq", PLANES * row_bytes + 4 * Q)
        slope = keep.tile([P, 1], F32, name="slope")
        nc.scalar.activation(slope[:], steep_col[:], ACT.Copy, scale=-1.0 / PAGE)
        shift = keep.tile([P, 1], F32, name="shift")
        nc.scalar.activation(shift[:], th_col[:], ACT.Copy, scale=steep_col[:])

        a = [psum.tile([P, I // 2], F32, name="a%d" % h) for h in range(2)]
        for h, cols in enumerate(halves):
            product(a[h][:], q_mx, (k_codes, k_scales), cols)
        ta = psum.tile([P, I], F32, name="ta")
        product(ta[:], dq_mx, (k_codes, k_scales))

        os_rows = psum.tile([P, PACK, P], F32, name="os_rows")
        for t in range(PACK):
            nc.tensor.transpose(os_rows[:, t, :], os_cols[:, t : t + 1].to_broadcast([P, P]), ident[:])

        def turn(rows, grouped, name, tag, copy=nc.scalar.copy):
            words = rows[:].bitcast(F32)
            turned = psum.tile([P, 2, P], F32, name="turned_" + name, tag=tag)
            for u in range(2):
                nc.tensor.transpose(turned[:, u, :], words[:, u : I // 2 : 2], ident[:])
            copy(
                grouped.bitcast(F32).rearrange("p (c u) -> p c u", u=2),
                turned[:].rearrange("p u c -> p c u"),
            )

        def gather_vals(j, grouped, tag, copy=nc.scalar.copy):
            picked = keep.tile([P, I], BF16, name="picked%d" % j, tag=tag, align_bytes=64)
            nc.vector.tensor_copy(picked[:], pools[j][:].indirect(offsets[:]))
            turn(picked, grouped, "v%d" % j, "turned_v%d" % j, copy)

        def paged(ap):
            return ap.rearrange("p (g j) -> p g j", j=PAGE)

        def spread(ap):
            return ap.unsqueeze(2).to_broadcast([P, G, PAGE])

        v01_grouped = keep.tile([P, 2 * I], BF16, name="v01_grouped", align_bytes=64)
        v2_grouped = keep.tile([P, I], BF16, name="v2_grouped", align_bytes=64)
        v3_grouped = keep.tile([P, I], BF16, name="v3_grouped", align_bytes=64)
        w_grouped = keep.tile([P, I], BF16, name="w_grouped", align_bytes=64)

        page_sum = keep.tile([P, G], F32, name="page_sum")
        neg_max_first = keep.tile([P, 1], F32, name="neg_max_first")
        neg_max = keep.tile([P, 1], F32, name="neg_max", tag="cast0", align_bytes=64)
        neg_a = keep.tile([P, I // 2], F32, name="neg_a")
        nc.vector.tensor_reduce(page_sum[:, 0 : G // 2], paged(a[0][:]), AX.X, ALU.add)
        nc.vector.tensor_reduce(neg_max_first[:], a[0][:], AX.X, ALU.max, negate=True)
        nc.vector.tensor_reduce(page_sum[:, G // 2 : G], paged(a[1][:]), AX.X, ALU.add)
        nc.vector.tensor_scalar(neg_a[:], a[1][:], -1.0, neg_max_first[:], ALU.mult, ALU.min, accum_out=neg_max[:])
        dpage_sum = keep.tile([P, G], F32, name="dpage_sum")
        nc.vector.tensor_reduce(dpage_sum[:], paged(ta[:]), AX.X, ALU.add)

        odds = keep.tile([P, G], F32, name="odds")
        nc.scalar.activation(odds[:], page_sum[:], ACT.Exp, bias=shift[:], scale=slope[:])
        denom = keep.tile([P, G], F32, name="denom")
        nc.scalar.activation(denom[:], odds[:], ACT.Identity, bias=one[:], scale=1.0)
        r = keep.tile([P, I], F32, name="r", tag="slot0", align_bytes=64)
        for h, cols in enumerate(halves):
            nc.scalar.activation(r[:, cols], a[h][:], ACT.Exp, bias=neg_max[:], scale=1.0)

        cast0 = keep.tile([P, T], BF16, name="cast0", tag="cast0", align_bytes=64)
        for c in range(0, T, 512):
            nc.scalar.activation(cast0[:, c : c + 512], pools[0][:, c : c + 512], ACT.Copy)
        picked0 = keep.tile([P, I], BF16, name="picked0", align_bytes=64)
        nc.scalar.activation(picked0[:], cast0[:].indirect(offsets[:]), ACT.Copy)

        gate = keep.tile([P, G], F32, name="gate")
        nc.vector.reciprocal(gate[:], denom[:])
        p = keep.tile([P, I], F32, name="p", tag="slot2", align_bytes=64)
        p_sum = keep.tile([P, 1], F32, name="p_sum")
        nc.vector.scalar_tensor_tensor(paged(p[:]), paged(r[:]), 1.0, spread(gate[:]), ALU.mult, ALU.mult, accum_out=p_sum[:])
        dgate = keep.tile([P, G], F32, name="dgate", tag="slot0", align_bytes=64)
        nc.vector.scalar_tensor_tensor(dgate[:], gate[:], 1.0, dpage_sum[:], ALU.subtract, ALU.mult)
        inv_sum = keep.tile([P, 1], F32, name="inv_sum")
        nc.vector.reciprocal(inv_sum[:], p_sum[:])
        z = keep.tile([P, I], F32, name="z")
        nc.vector.scalar_tensor_tensor(paged(z[:]), spread(dgate[:]), slope[:], paged(ta[:]), ALU.mult, ALU.add)
        p_os = keep.tile([P, I], F32, name="p_os")
        nc.vector.scalar_tensor_tensor(
            p_os[:].rearrange("q (p t) -> q p t", t=PACK), p[:].rearrange("q (p t) -> q p t", t=PACK), inv_sum[:],
            os_rows[:].rearrange("q t p -> q p t"), ALU.mult, ALU.mult,
        )
        tp = keep.tile([P, I], F32, name="tp", tag="slot3", align_bytes=64)
        mean_z = keep.tile([P, 1], F32, name="mean_z")
        nc.vector.scalar_tensor_tensor(tp[:], z[:], inv_sum[:], p[:], ALU.mult, ALU.mult, accum_out=mean_z[:])
        gather_vals(1, v01_grouped[:, I : 2 * I], "slot1")
        turn(picked0, v01_grouped[:, 0:I], "v0", "turned_v1")
        w = keep.tile([P, I], BF16, name="w", align_bytes=64)
        nc.vector.scalar_tensor_tensor(w[:], z[:], mean_z[:], p_os[:], ALU.subtract, ALU.mult)
        turn(w, w_grouped[:], "w", "turned_w")
        gather_vals(2, v2_grouped[:], "slot2")
        picked3 = keep.tile([P, I], BF16, name="picked3", tag="slot3", align_bytes=64)
        nc.vector.tensor_copy(picked3[:], pools[3][:].indirect(offsets[:]))
        w_mx = quantize(w_grouped[:], Q, "w", 3 * row_bytes)
        v01_mx = quantize(v01_grouped[:], 2 * P, "v01", 3 * row_bytes + 1024)
        v2_mx = quantize(v2_grouped[:], P, "v2", 3 * row_bytes + 2048)
        turn(picked3, v3_grouped[:], "v3", "turned_v3", nc.vector.tensor_copy)
        v3_mx = quantize(v3_grouped[:], P, "v3")

        for v_mx, lo, hi, tag in ((v01_mx, 0, 256, "a0"), (v2_mx, 256, 384, "ta"), (v3_mx, 384, 512, "a1")):
            acc = psum.tile([P, hi - lo], F32, name="out%d" % lo, tag=tag)
            product(acc[:], w_mx, v_mx)
            res = keep.tile([P, hi - lo], F32, name="res%d" % lo)
            nc.scalar.copy(res[:], acc[:])
            nc.sync.dma_start(out[:, lo:hi], res[:])
